import numpy as np
import ml_dtypes


def mxq(x, axis, fmt="e4m3"):
    dtype, down = {"e4m3": (ml_dtypes.float8_e4m3fn, 7), "e5m2": (ml_dtypes.float8_e5m2, 14)}[fmt]
    v = np.moveaxis(np.asarray(x, np.float32).astype(ml_dtypes.bfloat16).astype(np.float64), axis, -1)
    blocks = v.reshape(v.shape[:-1] + (-1, 32))
    amax = np.abs(blocks).max(-1, keepdims=True)
    byte = np.maximum(np.where(amax > 0, np.frexp(amax)[1] - 1 + 127, 0) - down, 1)
    scale = np.exp2(byte - 127.0)
    codes = (blocks / scale).astype(np.float32).astype(dtype).astype(np.float64)
    return np.moveaxis((codes * scale).reshape(v.shape), -1, axis)


WIDE = False


def mx_kscale(k):
    if not WIDE:
        return np.ones(k)
    levels = np.array([30, -30])
    if k % 512:
        return np.exp2(np.random.permutation(np.resize(levels, k // 32))).repeat(32)
    a = np.empty((k // 512, 16))
    for p in range(k // 512):
        a[p, :8] = np.random.permutation(np.resize(levels, 8))
        for g in range(8):
            far = levels[np.abs(levels - a[p, g]) >= 10]
            a[p, g + 8] = far[np.random.randint(len(far))]
    return np.exp2(a.ravel()).repeat(32)


def f64(x):
    return np.asarray(x).astype(np.float64)


def striped(idx):
    return np.tile(np.asarray(idx).reshape(-1, 16).T, (8, 1)).astype(np.uint16)


def unstriped(offs):
    return offs[:16].T.reshape(-1).astype(np.int64)


E2M1 = np.array([0.0, 0.5, 1.0, 1.5, 2.0, 3.0, 4.0, 6.0, -0.0, -0.5, -1.0, -1.5, -2.0, -3.0, -4.0, -6.0])


def pack_weight(w, fmt):
    k, n = w.shape
    w = f64(np.asarray(w, np.float32).astype(ml_dtypes.bfloat16)).reshape(k // 32, 32, n)
    amax = np.abs(w).max(1)
    if fmt == "e4m3":
        byte = np.frexp(amax)[1] - 1 + 127 - 7
    else:
        mant, ex = np.frexp(amax / 6.0)
        byte = np.where(mant > 0.5, ex, ex - 1) + 127
    byte = np.clip(np.where(amax > 0, byte, 1), 1, 254)
    scaled = (w * np.exp2(127.0 - byte)[:, None, :]).reshape(k, n).astype(np.float32)
    by_word = np.ascontiguousarray(scaled.reshape(k // 512, 128, 4, n).transpose(0, 1, 3, 2))
    if fmt == "e4m3":
        words = by_word.astype(ml_dtypes.float8_e4m3fn).view(np.uint8)
    else:
        c = by_word.astype(ml_dtypes.float4_e2m1fn).view(np.uint8) & 0xF
        words = (c[..., 0::2] | (c[..., 1::2] << 4)).reshape(k // 512, 128, 2 * n)
    return np.ascontiguousarray(words), np.ascontiguousarray(byte.astype(np.uint8).reshape(k // 512, 16, n))


def unpack_weight(words, scales, fmt):
    g, _, n = scales.shape
    words = np.ascontiguousarray(words).reshape(g, 128, n, -1)
    if fmt == "e4m3":
        vals = words.view(ml_dtypes.float8_e4m3fn).astype(np.float64)
    else:
        nib = np.empty((g, 128, n, 4), np.uint8)
        nib[..., 0::2] = words & 0xF
        nib[..., 1::2] = words >> 4
        vals = E2M1[nib]
    vals = vals * np.repeat(np.exp2(scales.astype(np.float64) - 127.0), 8, axis=1)[..., None]
    return vals.transpose(0, 1, 3, 2).reshape(g * 512, n)


N, K, T, J, I = 512, 512, 1024, 512, 512


def setup_inputs():
    n = np.random.standard_normal
    idx = np.random.permutation(T)[:J]
    idx2 = np.random.permutation(T)[:I]
    fn = mx_kscale(N)
    wap = pack_weight(n((N, K)) * 1 / np.sqrt(N) * fn[:, None], "e2m1")
    wbp = pack_weight(n((N, K)) * 1 / np.sqrt(N) * fn[:, None], "e4m3")
    return {
        "g": (n((N, T)) * np.exp(0.5 * n((1, T))) / fn[:, None]).astype(np.float32),
        "wa_words": wap[0],
        "wa_scales": wap[1],
        "wb_words": wbp[0],
        "wb_scales": wbp[1],
        "ga": (np.random.uniform(0.4, 1.2, (1, J))).astype(np.float32),
        "gb": (np.random.uniform(0.4, 1.2, (1, I))).astype(np.float32),
        "run": (0.3 * n((K, T))).astype(np.float32),
        "offs": striped(idx),
        "offs2": striped(idx2),
    }


def reference(g, wa_words, wa_scales, wb_words, wb_scales, ga, gb, run, offs, offs2):
    idx = unstriped(offs)
    idx2 = unstriped(offs2)
    wau = unpack_weight(wa_words, wa_scales, "e2m1")
    wbu = unpack_weight(wb_words, wb_scales, "e4m3")
    u = f64(g)[:, idx] * f64(ga)
    v = f64(g)[:, idx2] * f64(gb)
    uq = mxq(u, 0, "e5m2")
    p = wau.T @ uq
    vq = mxq(v, 0, "e5m2")
    q = wbu.T @ vq
    pg = np.zeros((K, T))
    pg[:, idx] = p
    qg = np.zeros((K, T))
    qg[:, idx2] = q
    y = pg + qg + f64(run)
    return y

@@ -1,0 +1,220 @@
+from contextlib import ExitStack
+
+import concourse.mybir as mybir
+from concourse.masks import make_identity
+
+F32 = mybir.dt.float32
+BF16 = mybir.dt.bfloat16
+I32 = mybir.dt.int32
+U32 = mybir.dt.uint32
+U16 = mybir.dt.uint16
+U8 = mybir.dt.uint8
+FP4X4 = mybir.dt.float4_e2m1fn_x4
+E4M3X4 = mybir.dt.float8_e4m3fn_x4
+E5M2X4 = mybir.dt.float8_e5m2_x4
+MULT = mybir.AluOpType.mult
+ADD = mybir.AluOpType.add
+
+N, K, T, S = 512, 512, 1024, 512
+P = 128
+PACK = 4
+BANK = 512
+FLOPS = 2 * 2 * N * K * S
+
+
+def tile_moe_experts_input_gradient_two_kernel(
+    tc, g, wa_words, wa_scales, wb_words, wb_scales, ga, gb, run, offs, offs2, out
+):
+    nc = tc.nc
+    with ExitStack() as ctx:
+        keep = ctx.enter_context(tc.tile_pool(name="keep", bufs=1))
+        psum = ctx.enter_context(tc.psum_pool(name="psum", bufs=1))
+
+        def sb(name, shape, dtype):
+            return keep.tile(shape, dtype, name=name, align_bytes=64)
+
+        list_a = keep.tile([P, S // 16], U16, name="list_a")
+        list_b = keep.tile([P, S // 16], U16, name="list_b")
+        g_rows = [sb("g_rows%d" % r, [P, T], F32) for r in range(PACK)]
+        run_rows = [sb("run_rows%d" % kt, [P, T], F32) for kt in range(K // P)]
+        gate_cols = [sb("gate_cols%d" % e, [P, PACK], F32) for e in range(2)]
+        gate = [sb("gate%d" % e, [P, S], F32) for e in range(2)]
+        wa_sb = sb("wa_sb", [P, 2 * K], U8)
+        wb_sb = sb("wb_sb", [P, K], U32)
+        w_scales = sb("w_scales", [P, 2 * K], U8)
+        identity = sb("identity", [P, P], F32)
+        places = [sb("places%d" % i, [P, T], F32) for i in range(4)]
+        u_f32 = sb("u_f32", [P, PACK * S], F32)
+        v_f32 = sb("v_f32", [P, PACK * S], F32)
+        u_bf16 = v_f32[:, 2 * S : 4 * S].bitcast(BF16)
+        v_bf16 = sb("v_bf16", [P, PACK * S], BF16)
+        codes = [sb("codes%d" % e, [P, S], U32) for e in range(2)]
+        scales = [sb("scales%d" % e, [P, S], U8) for e in range(2)]
+        staged0 = sb("staged0", [P, S], F32)
+        staged = [staged0[:], v_f32[:, 0:S]]
+        turned = [sb("turned%d" % h, [P, BANK], F32) for h in range(2)]
+        result = [[sb("result%d_%d" % (kt, h), [P, BANK], F32) for h in range(2)] for kt in range(K // P)]
+
+        mx_bank = [psum.tile([P, BANK], F32, name="mx_bank%d" % i) for i in range(4)]
+        sum_bank = [psum.tile([P, BANK], F32, name="sum_bank%d" % h) for h in range(2)]
+        back_bank = [psum.tile([P, BANK], F32, name="back_bank%d" % h) for h in range(2)]
+
+        nc.vector.memset(w_scales[:].bitcast(U32), 0)
+        make_identity(nc, identity[:])
+        for w in places:
+            nc.vector.memset(w[:], 0.0)
+
+        g_view = g.rearrange("(p r) t -> r p t", r=PACK)
+        nc.scalar.dma_start(gate_cols[0][:], ga.rearrange("o (p c) -> (o p) c", c=PACK))
+        nc.scalar.dma_start(gate_cols[1][:], gb.rearrange("o (p c) -> (o p) c", c=PACK))
+        nc.sync.dma_start(list_a[:], offs)
+        for r in range(PACK):
+            nc.sync.dma_start(g_rows[r][:], g_view[r])
+        nc.sync.dma_start(list_b[:], offs2)
+
+        def load_scales(e, dram):
+            rows = dram[0].bitcast(I32).rearrange("(q r) c -> r q c", r=4)
+            plane = w_scales[:, e * K : (e + 1) * K].bitcast(I32)
+            for r in range(4):
+                nc.sync.dma_start(plane[r:P:32, :], rows[r])
+
+        nc.sync.dma_start(wa_sb[:].bitcast(I32), wa_words[0].bitcast(I32))
+        load_scales(0, wa_scales)
+        nc.sync.dma_start(wb_sb[:].bitcast(I32), wb_words[0].rearrange("p n r -> p (n r)").bitcast(I32))
+        load_scales(1, wb_scales)
+        for kt in range(K // P):
+            nc.sync.dma_start(run_rows[kt][:], run[kt * P : (kt + 1) * P, :])
+
+        def spread_gate(e):
+            bank = back_bank[e]
+            for c in range(PACK):
+                nc.tensor.transpose(
+                    bank[:, c * P : (c + 1) * P], gate_cols[e][:, c : c + 1].to_broadcast([P, P]), identity[:]
+                )
+            nc.scalar.copy(
+                gate[e][:].rearrange("p (n c) -> p n c", c=PACK), bank[:].rearrange("p (c n) -> p n c", c=PACK)
+            )
+
+        def gather(dst, e, lst, r, lo, hi):
+            nc.vector.tensor_tensor(
+                dst[:, r * S + lo : r * S + hi],
+                g_rows[r][:].indirect(lst[:, lo // 16 : hi // 16]),
+                gate[e][:, lo:hi],
+                MULT,
+            )
+
+        def weave(dst, src, lo, hi):
+            a, b = lo // 4, hi // 4
+            nc.scalar.copy(
+                dst.rearrange("p (c i r) -> p c r i", i=4, r=PACK)[:, a:b],
+                src[:].rearrange("p (r c i) -> p c r i", i=4, r=PACK)[:, a:b],
+            )
+
+        def quantise(e, src):
+            nc.vector.quantize_mx(out=codes[e][:].bitcast(E5M2X4), scales=scales[e][:], in_=src)
+
+        def product(e, kt, bank):
+            if e == 0:
+                w = wa_sb[:, 2 * kt * P : 2 * (kt + 1) * P].bitcast(FP4X4)
+            else:
+                w = wb_sb[:, kt * P : (kt + 1) * P].bitcast(E4M3X4)
+            nc.tensor.matmul_mx(
+                out=bank[:],
+                lhsT=w,
+                lhsT_scale=w_scales[:, e * K + kt * P : e * K + (kt + 1) * P],
+                rhs=codes[e][:].bitcast(E5M2X4),
+                rhs_scale=scales[e][:],
+                start=True,
+                stop=True,
+            )
+
+        def stage(i, bank):
+            nc.scalar.copy(staged[i % 2], bank[:])
+
+        def scatter(i, e, kt):
+            lst = list_a if e == 0 else list_b
+            nc.vector.tensor_copy(places[2 * e + kt % 2][:].indirect(lst[:]), staged[i % 2])
+
+        def add_turned(src, first, last):
+            for h in range(2):
+                for b in range(4):
+                    col = h * BANK + b * P
+                    nc.tensor.matmul(
+                        sum_bank[h][:, b * P : (b + 1) * P],
+                        src[:, col : col + P],
+                        identity[:],
+                        is_transpose=True,
+                        start=(first and b == 0),
+                        stop=(last and b == 3),
+                    )
+
+        def turn_back():
+            for h in range(2):
+                nc.scalar.copy(turned[h][:], sum_bank[h][:])
+                for b in range(4):
+                    nc.tensor.transpose(
+                        back_bank[h][:, b * P : (b + 1) * P], turned[h][:, b * P : (b + 1) * P], identity[:]
+                    )
+
+        def finish(kt):
+            add_turned(places[2 + kt % 2], False, True)
+            turn_back()
+            for h in range(2):
+                nc.scalar.copy(result[kt][h][:], back_bank[h][:])
+                nc.sync.dma_start(out[kt * P : (kt + 1) * P, h * BANK : (h + 1) * BANK], result[kt][h][:])
+
+        def begin(kt, last):
+            add_turned(run_rows[kt], True, False)
+            add_turned(places[kt % 2], False, last)
+
+        spread_gate(0)
+        spread_gate(1)
+        for r in range(PACK - 1):
+            gather(u_f32, 0, list_a, r, 0, S)
+        for lo in (0, S // 2):
+            gather(u_f32, 0, list_a, PACK - 1, lo, lo + S // 2)
+            weave(u_bf16, u_f32, lo, lo + S // 2)
+        for r in range(2):
+            gather(v_f32, 1, list_b, r, 0, S)
+        quantise(0, u_bf16)
+        for r in range(2, PACK):
+            gather(v_f32, 1, list_b, r, 0, S)
+        for kt in range(3):
+            product(0, kt, mx_bank[kt])
+        stage(0, mx_bank[0])
+        weave(v_bf16[:], v_f32, 0, S)
+        scatter(0, 0, 0)
+        quantise(1, v_bf16[:])
+        stage(1, mx_bank[1])
+        scatter(1, 0, 1)
+        product(1, 0, mx_bank[3])
+        product(1, 1, mx_bank[0])
+        begin(0, False)
+        stage(2, mx_bank[3])
+        scatter(2, 1, 0)
+        stage(3, mx_bank[0])
+        scatter(3, 1, 1)
+        stage(4, mx_bank[2])
+        finish(0)
+        scatter(4, 0, 2)
+        product(1, 2, back_bank[1])
+        stage(5, back_bank[1])
+        begin(1, False)
+        finish(1)
+        scatter(5, 1, 2)
+        product(0, 3, back_bank[1])
+        stage(6, back_bank[1])
+        begin(2, False)
+        scatter(6, 0, 3)
+        product(1, 3, back_bank[1])
+        stage(7, back_bank[1])
+        finish(2)
+        scatter(7, 1, 3)
+        begin(3, True)
+        turn_back()
+        for h in range(2):
+            nc.vector.tensor_tensor(
+                result[3][h][:], back_bank[h][:], places[3][:, h * BANK : (h + 1) * BANK], ADD
+            )
+            queue = nc.sync if h == 0 else nc.scalar
+            queue.dma_start(out[3 * P : 4 * P, h * BANK : (h + 1) * BANK], result[3][h][:])

@@ -30,8 +30,8 @@ def tile_moe_experts_input_gradient_two_kernel(
         keep = ctx.enter_context(tc.tile_pool(name="keep", bufs=1))
         psum = ctx.enter_context(tc.psum_pool(name="psum", bufs=1))
 
-        def sb(name, shape, dtype):
-            return keep.tile(shape, dtype, name=name, align_bytes=64)
+        def sb(name, shape, dtype, tag=None):
+            return keep.tile(shape, dtype, name=name, tag=tag or name, align_bytes=64)
 
         list_a = keep.tile([P, S // 16], U16, name="list_a")
         list_b = keep.tile([P, S // 16], U16, name="list_b")
@@ -50,18 +50,23 @@ def tile_moe_experts_input_gradient_two_kernel(
         v_bf16 = sb("v_bf16", [P, PACK * S], BF16)
         codes = [sb("codes%d" % e, [P, S], U32) for e in range(2)]
         scales = [sb("scales%d" % e, [P, S], U8) for e in range(2)]
-        staged0 = sb("staged0", [P, S], F32)
-        staged = [staged0[:], v_f32[:, 0:S]]
-        turned = [sb("turned%d" % h, [P, BANK], F32) for h in range(2)]
+        staged = {}
+        for e in range(2):
+            for kt in range(K // P):
+                if e == 0 and kt in (1, 2):
+                    staged[e, kt] = v_f32[:, (kt - 1) * S : kt * S]
+                else:
+                    staged[e, kt] = sb("staged%d_%d" % (e, kt), [P, S], F32)[:]
+        turned = [[sb("turned%d_%d" % (kt, h), [P, BANK], F32) for h in range(2)] for kt in range(K // P)]
         result = [[sb("result%d_%d" % (kt, h), [P, BANK], F32) for h in range(2)] for kt in range(K // P)]
 
-        mx_bank = [psum.tile([P, BANK], F32, name="mx_bank%d" % i) for i in range(4)]
-        sum_bank = [psum.tile([P, BANK], F32, name="sum_bank%d" % h) for h in range(2)]
-        back_bank = [psum.tile([P, BANK], F32, name="back_bank%d" % h) for h in range(2)]
+        banks = [[psum.tile([P, BANK], F32, name="bank%d_%d" % (kt, h)) for h in range(2)] for kt in range(K // P)]
 
         nc.vector.memset(w_scales[:].bitcast(U32), 0)
         make_identity(nc, identity[:])
-        for w in places:
+        for w in places[:2]:
+            nc.gpsimd.memset(w[:], 0.0)
+        for w in places[2:]:
             nc.vector.memset(w[:], 0.0)
 
         g_view = g.rearrange("(p r) t -> r p t", r=PACK)
@@ -86,7 +91,7 @@ def tile_moe_experts_input_gradient_two_kernel(
             nc.sync.dma_start(run_rows[kt][:], run[kt * P : (kt + 1) * P, :])
 
         def spread_gate(e):
-            bank = back_bank[e]
+            bank = banks[0][e]
             for c in range(PACK):
                 nc.tensor.transpose(
                     bank[:, c * P : (c + 1) * P], gate_cols[e][:, c : c + 1].to_broadcast([P, P]), identity[:]
@@ -128,44 +133,44 @@ def tile_moe_experts_input_gradient_two_kernel(
                 stop=True,
             )
 
-        def stage(i, bank):
-            nc.scalar.copy(staged[i % 2], bank[:])
+        def stage(e, kt, bank):
+            product(e, kt, bank)
+            nc.scalar.copy(staged[e, kt], bank[:])
 
-        def scatter(i, e, kt):
+        def scatter(e, kt):
             lst = list_a if e == 0 else list_b
-            nc.vector.tensor_copy(places[2 * e + kt % 2][:].indirect(lst[:]), staged[i % 2])
+            nc.vector.tensor_copy(places[2 * e + kt % 2][:].indirect(lst[:]), staged[e, kt])
 
-        def add_turned(src, first, last):
+        def add_turned(kt, src, ident, first, last):
             for h in range(2):
                 for b in range(4):
                     col = h * BANK + b * P
                     nc.tensor.matmul(
-                        sum_bank[h][:, b * P : (b + 1) * P],
+                        banks[kt][h][:, b * P : (b + 1) * P],
                         src[:, col : col + P],
-                        identity[:],
+                        ident[:],
                         is_transpose=True,
                         start=(first and b == 0),
                         stop=(last and b == 3),
                     )
 
-        def turn_back():
+        def identity_over(tag):
+            copy = sb("identity_" + tag, [P, P], F32, tag=tag)
+            nc.scalar.copy(copy[:], identity[:])
+            return copy
+
+        def turn_back(kt):
             for h in range(2):
-                nc.scalar.copy(turned[h][:], sum_bank[h][:])
+                nc.scalar.copy(turned[kt][h][:], banks[kt][h][:])
                 for b in range(4):
                     nc.tensor.transpose(
-                        back_bank[h][:, b * P : (b + 1) * P], turned[h][:, b * P : (b + 1) * P], identity[:]
+                        banks[kt][h][:, b * P : (b + 1) * P], turned[kt][h][:, b * P : (b + 1) * P], identity[:]
                     )
 
-        def finish(kt):
-            add_turned(places[2 + kt % 2], False, True)
-            turn_back()
+        def store(kt):
             for h in range(2):
-                nc.scalar.copy(result[kt][h][:], back_bank[h][:])
+                nc.scalar.copy(result[kt][h][:], banks[kt][h][:])
                 nc.sync.dma_start(out[kt * P : (kt + 1) * P, h * BANK : (h + 1) * BANK], result[kt][h][:])
-
-        def begin(kt, last):
-            add_turned(run_rows[kt], True, False)
-            add_turned(places[kt % 2], False, last)
 
         spread_gate(0)
         spread_gate(1)
@@ -179,42 +184,50 @@ def tile_moe_experts_input_gradient_two_kernel(
         quantise(0, u_bf16)
         for r in range(2, PACK):
             gather(v_f32, 1, list_b, r, 0, S)
-        for kt in range(3):
-            product(0, kt, mx_bank[kt])
-        stage(0, mx_bank[0])
+        spare = banks[3]
+        stage(0, 0, spare[0])
+        product(0, 1, spare[1])
         weave(v_bf16[:], v_f32, 0, S)
-        scatter(0, 0, 0)
+        scatter(0, 0)
         quantise(1, v_bf16[:])
-        stage(1, mx_bank[1])
-        scatter(1, 0, 1)
-        product(1, 0, mx_bank[3])
-        product(1, 1, mx_bank[0])
-        begin(0, False)
-        stage(2, mx_bank[3])
-        scatter(2, 1, 0)
-        stage(3, mx_bank[0])
-        scatter(3, 1, 1)
-        stage(4, mx_bank[2])
-        finish(0)
-        scatter(4, 0, 2)
-        product(1, 2, back_bank[1])
-        stage(5, back_bank[1])
-        begin(1, False)
-        finish(1)
-        scatter(5, 1, 2)
-        product(0, 3, back_bank[1])
-        stage(6, back_bank[1])
-        begin(2, False)
-        scatter(6, 0, 3)
-        product(1, 3, back_bank[1])
-        stage(7, back_bank[1])
-        finish(2)
-        scatter(7, 1, 3)
-        begin(3, True)
-        turn_back()
+        nc.scalar.copy(staged[0, 1], spare[1][:])
+        scatter(0, 1)
+        stage(0, 2, spare[0])
+        stage(1, 0, spare[1])
+        stage(1, 1, spare[0])
+        stage(1, 2, spare[1])
+        for kt in range(3):
+            add_turned(kt, run_rows[kt], identity, True, False)
+        add_turned(0, places[0], identity, False, False)
+        scatter(0, 2)
+        add_turned(1, places[1], identity, False, False)
+        scatter(1, 0)
+        add_turned(2, places[0], identity, False, False)
+        add_turned(3, run_rows[3], identity, True, False)
+        ident = identity_over("run_rows3")
+        scatter(1, 1)
+        add_turned(0, places[2], ident, False, True)
+        scatter(1, 2)
+        turn_back(0)
+        ident = identity_over("turned0_0")
+        store(0)
+        stage(0, 3, banks[0][0])
+        stage(1, 3, banks[0][0])
+        add_turned(1, places[3], ident, False, True)
+        scatter(0, 3)
+        scatter(1, 3)
+        turn_back(1)
+        ident = identity_over("turned1_0")
+        store(1)
+        add_turned(2, places[2], ident, False, True)
+        turn_back(2)
+        ident = identity_over("turned2_0")
+        store(2)
+        add_turned(3, places[1], ident, False, True)
+        turn_back(3)
         for h in range(2):
             nc.vector.tensor_tensor(
-                result[3][h][:], back_bank[h][:], places[3][:, h * BANK : (h + 1) * BANK], ADD
+                result[3][h][:], banks[3][h][:], places[3][:, h * BANK : (h + 1) * BANK], ADD
             )
             queue = nc.sync if h == 0 else nc.scalar
             queue.dma_start(out[3 * P : 4 * P, h * BANK : (h + 1) * BANK], result[3][h][:])

@@ -19,6 +19,8 @@ N, K, T, S = 512, 512, 1024, 512
 P = 128
 PACK = 4
 BANK = 512
+FIRST = 192
+LATE = 16
 FLOPS = 2 * 2 * N * K * S
 
 
@@ -43,21 +45,26 @@ def tile_moe_experts_input_gradient_two_kernel(
         wb_sb = sb("wb_sb", [P, K], U32)
         w_scales = sb("w_scales", [P, 2 * K], U8)
         identity = sb("identity", [P, P], F32)
-        places = [sb("places%d" % i, [P, T], F32) for i in range(4)]
+        places = [sb("places%d" % i, [P, T], F32) for i in range(5)]
         u_f32 = sb("u_f32", [P, PACK * S], F32)
         v_f32 = sb("v_f32", [P, PACK * S], F32)
         u_bf16 = v_f32[:, 2 * S : 4 * S].bitcast(BF16)
         v_bf16 = sb("v_bf16", [P, PACK * S], BF16)
         codes = [sb("codes%d" % e, [P, S], U32) for e in range(2)]
         scales = [sb("scales%d" % e, [P, S], U8) for e in range(2)]
+        shared = sb("shared", [P, 2, S - LATE + BANK], F32)
+        late_part = sb("late_part", [P, 2, LATE], F32)
         staged = {}
         for e in range(2):
             for kt in range(K // P):
                 if e == 0 and kt in (1, 2):
                     staged[e, kt] = v_f32[:, (kt - 1) * S : kt * S]
+                elif kt == 3:
+                    staged[e, kt] = shared[:, e, 0:S]
                 else:
                     staged[e, kt] = sb("staged%d_%d" % (e, kt), [P, S], F32)[:]
-        turned = [[sb("turned%d_%d" % (kt, h), [P, BANK], F32) for h in range(2)] for kt in range(K // P)]
+        turned = [[sb("turned%d_%d" % (kt, h), [P, BANK], F32)[:] for h in range(2)] for kt in range(K // P)]
+        turned[0][1] = shared[:, 0, S - LATE :]
         result = [[sb("result%d_%d" % (kt, h), [P, BANK], F32) for h in range(2)] for kt in range(K // P)]
 
         banks = [[psum.tile([P, BANK], F32, name="bank%d_%d" % (kt, h)) for h in range(2)] for kt in range(K // P)]
@@ -90,15 +97,17 @@ def tile_moe_experts_input_gradient_two_kernel(
         for kt in range(K // P):
             nc.sync.dma_start(run_rows[kt][:], run[kt * P : (kt + 1) * P, :])
 
-        def spread_gate(e):
+        def spread_gate(e, pieces):
             bank = banks[0][e]
             for c in range(PACK):
                 nc.tensor.transpose(
                     bank[:, c * P : (c + 1) * P], gate_cols[e][:, c : c + 1].to_broadcast([P, P]), identity[:]
                 )
-            nc.scalar.copy(
-                gate[e][:].rearrange("p (n c) -> p n c", c=PACK), bank[:].rearrange("p (c n) -> p n c", c=PACK)
-            )
+            for lo, hi in pieces:
+                nc.scalar.copy(
+                    gate[e][:].rearrange("p (n c) -> p n c", c=PACK)[:, lo // PACK : hi // PACK],
+                    bank[:].rearrange("p (c n) -> p n c", c=PACK)[:, lo // PACK : hi // PACK],
+                )
 
         def gather(dst, e, lst, r, lo, hi):
             nc.vector.tensor_tensor(
@@ -137,9 +146,13 @@ def tile_moe_experts_input_gradient_two_kernel(
             product(e, kt, bank)
             nc.scalar.copy(staged[e, kt], bank[:])
 
+        def stage_but_last(e, bank):
+            nc.scalar.copy(staged[e, 3][:, : S - LATE], bank[:, : S - LATE])
+            nc.scalar.copy(late_part[:, e, :], bank[:, S - LATE :])
+
         def scatter(e, kt):
             lst = list_a if e == 0 else list_b
-            nc.vector.tensor_copy(places[2 * e + kt % 2][:].indirect(lst[:]), staged[e, kt])
+            nc.vector.tensor_copy(places[4 if (e, kt) == (0, 2) else 2 * e + kt % 2][:].indirect(lst[:]), staged[e, kt])
 
         def add_turned(kt, src, ident, first, last):
             for h in range(2):
@@ -161,7 +174,7 @@ def tile_moe_experts_input_gradient_two_kernel(
 
         def turn_back(kt):
             for h in range(2):
-                nc.scalar.copy(turned[kt][h][:], banks[kt][h][:])
+                nc.scalar.copy(turned[kt][h], banks[kt][h][:])
                 for b in range(4):
                     nc.tensor.transpose(
                         banks[kt][h][:, b * P : (b + 1) * P], turned[kt][h][:, b * P : (b + 1) * P], identity[:]
@@ -172,37 +185,47 @@ def tile_moe_experts_input_gradient_two_kernel(
                 nc.scalar.copy(result[kt][h][:], banks[kt][h][:])
                 nc.sync.dma_start(out[kt * P : (kt + 1) * P, h * BANK : (h + 1) * BANK], result[kt][h][:])
 
-        spread_gate(0)
-        spread_gate(1)
-        for r in range(PACK - 1):
-            gather(u_f32, 0, list_a, r, 0, S)
+        first_pieces = ((0, FIRST), (FIRST, S))
+        spread_gate(0, first_pieces)
+        spread_gate(1, ((0, S),))
+        for lo, hi in first_pieces:
+            gather(u_f32, 0, list_a, 0, lo, hi)
+        gather(u_f32, 0, list_a, 1, 0, S)
         for lo in (0, S // 2):
-            gather(u_f32, 0, list_a, PACK - 1, lo, lo + S // 2)
+            for r in (2, 3):
+                gather(u_f32, 0, list_a, r, lo, lo + S // 2)
             weave(u_bf16, u_f32, lo, lo + S // 2)
         for r in range(2):
             gather(v_f32, 1, list_b, r, 0, S)
         quantise(0, u_bf16)
-        for r in range(2, PACK):
-            gather(v_f32, 1, list_b, r, 0, S)
+        gather(v_f32, 1, list_b, 2, 0, S)
+        for lo in (0, S // 2):
+            gather(v_f32, 1, list_b, 3, lo, lo + S // 2)
         spare = banks[3]
         stage(0, 0, spare[0])
         product(0, 1, spare[1])
-        weave(v_bf16[:], v_f32, 0, S)
+        product(0, 2, spare[0])
+        for lo in (0, S // 2):
+            weave(v_bf16[:], v_f32, lo, lo + S // 2)
         scatter(0, 0)
         quantise(1, v_bf16[:])
         nc.scalar.copy(staged[0, 1], spare[1][:])
         scatter(0, 1)
-        stage(0, 2, spare[0])
-        stage(1, 0, spare[1])
-        stage(1, 1, spare[0])
-        stage(1, 2, spare[1])
+        nc.scalar.copy(staged[0, 2], spare[0][:])
+        product(0, 3, spare[1])
+        stage_but_last(0, spare[1])
         for kt in range(3):
             add_turned(kt, run_rows[kt], identity, True, False)
         add_turned(0, places[0], identity, False, False)
+        for kt in range(3):
+            stage(1, kt, spare[kt % 2])
+        product(1, 3, spare[1])
+        stage_but_last(1, spare[1])
+        ident = identity_over("wb_sb")
         scatter(0, 2)
-        add_turned(1, places[1], identity, False, False)
+        add_turned(1, places[1], ident, False, False)
+        add_turned(2, places[4], ident, False, False)
         scatter(1, 0)
-        add_turned(2, places[0], identity, False, False)
         add_turned(3, run_rows[3], identity, True, False)
         ident = identity_over("run_rows3")
         scatter(1, 1)
@@ -210,9 +233,8 @@ def tile_moe_experts_input_gradient_two_kernel(
         scatter(1, 2)
         turn_back(0)
         ident = identity_over("turned0_0")
+        nc.scalar.copy(shared[:, :, S - LATE : S], late_part[:])
         store(0)
-        stage(0, 3, banks[0][0])
-        stage(1, 3, banks[0][0])
         add_turned(1, places[3], ident, False, True)
         scatter(0, 3)
         scatter(1, 3)
@@ -225,9 +247,7 @@ def tile_moe_experts_input_gradient_two_kernel(
         store(2)
         add_turned(3, places[1], ident, False, True)
         turn_back(3)
-        for h in range(2):
-            nc.vector.tensor_tensor(
-                result[3][h][:], banks[3][h][:], places[3][:, h * BANK : (h + 1) * BANK], ADD
-            )
-            queue = nc.sync if h == 0 else nc.scalar
-            queue.dma_start(out[3 * P : 4 * P, h * BANK : (h + 1) * BANK], result[3][h][:])
+        for h, lo, hi, queue in ((0, 0, BANK, nc.sync), (1, 0, BANK // 2, nc.scalar), (1, BANK // 2, BANK, nc.sync)):
+            cols = slice(h * BANK + lo, h * BANK + hi)
+            nc.vector.tensor_tensor(result[3][h][:, lo:hi], banks[3][h][:, lo:hi], places[3][:, cols], ADD)
+            queue.dma_start(out[3 * P : 4 * P, cols], result[3][h][:, lo:hi])

@@ -14,12 +14,12 @@ E4M3X4 = mybir.dt.float8_e4m3fn_x4
 E5M2X4 = mybir.dt.float8_e5m2_x4
 MULT = mybir.AluOpType.mult
 ADD = mybir.AluOpType.add
+COPY = mybir.ActivationFunctionType.Copy
 
 N, K, T, S = 512, 512, 1024, 512
 P = 128
 PACK = 4
 BANK = 512
-FIRST = 192
 LATE = 16
 FLOPS = 2 * 2 * N * K * S
 
@@ -45,10 +45,12 @@ def tile_moe_experts_input_gradient_two_kernel(
         wb_sb = sb("wb_sb", [P, K], U32)
         w_scales = sb("w_scales", [P, 2 * K], U8)
         identity = sb("identity", [P, P], F32)
-        places = [sb("places%d" % i, [P, T], F32) for i in range(5)]
+        places = {i: sb("places%d" % i, [P, T], F32) for i in (0, 2, 3)}
+        v0_plain = sb("v0_plain", [P, S], F32)
+        v0_gated = sb("v0_gated", [P, S], F32)
         u_f32 = sb("u_f32", [P, PACK * S], F32)
-        v_f32 = sb("v_f32", [P, PACK * S], F32)
-        u_bf16 = v_f32[:, 2 * S : 4 * S].bitcast(BF16)
+        v_f32 = sb("v_f32", [P, PACK * S + S // 2], F32)
+        u_bf16 = v_f32[:, 2 * S + S // 2 :].bitcast(BF16)
         v_bf16 = sb("v_bf16", [P, PACK * S], BF16)
         codes = [sb("codes%d" % e, [P, S], U32) for e in range(2)]
         scales = [sb("scales%d" % e, [P, S], U8) for e in range(2)]
@@ -71,18 +73,18 @@ def tile_moe_experts_input_gradient_two_kernel(
 
         nc.vector.memset(w_scales[:].bitcast(U32), 0)
         make_identity(nc, identity[:])
-        for w in places[:2]:
-            nc.gpsimd.memset(w[:], 0.0)
-        for w in places[2:]:
-            nc.vector.memset(w[:], 0.0)
+        nc.gpsimd.memset(places[0][:], 0.0)
+        for i in (2, 3):
+            nc.vector.memset(places[i][:], 0.0)
 
         g_view = g.rearrange("(p r) t -> r p t", r=PACK)
         nc.scalar.dma_start(gate_cols[0][:], ga.rearrange("o (p c) -> (o p) c", c=PACK))
         nc.scalar.dma_start(gate_cols[1][:], gb.rearrange("o (p c) -> (o p) c", c=PACK))
-        nc.sync.dma_start(list_a[:], offs)
-        for r in range(PACK):
-            nc.sync.dma_start(g_rows[r][:], g_view[r])
         nc.sync.dma_start(list_b[:], offs2)
+        nc.sync.dma_start(g_rows[0][:], g_view[0])
+        nc.sync.dma_start(list_a[:], offs)
+        for r in range(1, PACK):
+            nc.sync.dma_start(g_rows[r][:], g_view[r])
 
         def load_scales(e, dram):
             rows = dram[0].bitcast(I32).rearrange("(q r) c -> r q c", r=4)
@@ -97,17 +99,15 @@ def tile_moe_experts_input_gradient_two_kernel(
         for kt in range(K // P):
             nc.sync.dma_start(run_rows[kt][:], run[kt * P : (kt + 1) * P, :])
 
-        def spread_gate(e, pieces):
+        def spread_gate(e):
             bank = banks[0][e]
             for c in range(PACK):
                 nc.tensor.transpose(
                     bank[:, c * P : (c + 1) * P], gate_cols[e][:, c : c + 1].to_broadcast([P, P]), identity[:]
                 )
-            for lo, hi in pieces:
-                nc.scalar.copy(
-                    gate[e][:].rearrange("p (n c) -> p n c", c=PACK)[:, lo // PACK : hi // PACK],
-                    bank[:].rearrange("p (c n) -> p n c", c=PACK)[:, lo // PACK : hi // PACK],
-                )
+            nc.scalar.copy(
+                gate[e][:].rearrange("p (n c) -> p n c", c=PACK), bank[:].rearrange("p (c n) -> p n c", c=PACK)
+            )
 
         def gather(dst, e, lst, r, lo, hi):
             nc.vector.tensor_tensor(
@@ -121,7 +121,7 @@ def tile_moe_experts_input_gradient_two_kernel(
             a, b = lo // 4, hi // 4
             nc.scalar.copy(
                 dst.rearrange("p (c i r) -> p c r i", i=4, r=PACK)[:, a:b],
-                src[:].rearrange("p (r c i) -> p c r i", i=4, r=PACK)[:, a:b],
+                src[:, : PACK * S].rearrange("p (r c i) -> p c r i", i=4, r=PACK)[:, a:b],
             )
 
         def quantise(e, src):
@@ -185,20 +185,35 @@ def tile_moe_experts_input_gradient_two_kernel(
                 nc.scalar.copy(result[kt][h][:], banks[kt][h][:])
                 nc.sync.dma_start(out[kt * P : (kt + 1) * P, h * BANK : (h + 1) * BANK], result[kt][h][:])
 
-        first_pieces = ((0, FIRST), (FIRST, S))
-        spread_gate(0, first_pieces)
-        spread_gate(1, ((0, S),))
-        for lo, hi in first_pieces:
-            gather(u_f32, 0, list_a, 0, lo, hi)
-        gather(u_f32, 0, list_a, 1, 0, S)
+        spread_gate(0)
+        spread_gate(1)
+        nc.vector.tensor_copy(v0_plain[:], g_rows[0][:].indirect(list_b[:]))
+        there, back = banks[1]
+        for c in range(PACK):
+            nc.tensor.transpose(there[:, c * P : (c + 1) * P], v0_plain[:, c:S:PACK], identity[:])
+        for c in range(PACK):
+            nc.scalar.activation(
+                v0_gated[:, c * P : (c + 1) * P], there[:, c * P : (c + 1) * P], COPY, scale=gate_cols[1][:, c : c + 1]
+            )
+        for c in range(PACK):
+            nc.tensor.transpose(back[:, c * P : (c + 1) * P], v0_gated[:, c * P : (c + 1) * P], identity[:])
+        nc.scalar.copy(
+            v_f32[:, 0:S].rearrange("p (n c) -> p n c", c=PACK), back[:].rearrange("p (c n) -> p n c", c=PACK)
+        )
+        places[1] = sb("places1", [P, T], F32, tag="v0_plain")
+        places[4] = sb("places4", [P, T], F32, tag="v0_gated")
+        for i in (1, 4):
+            nc.gpsimd.memset(places[i][:], 0.0)
+        for r in range(2):
+            gather(u_f32, 0, list_a, r, 0, S)
         for lo in (0, S // 2):
             for r in (2, 3):
                 gather(u_f32, 0, list_a, r, lo, lo + S // 2)
             weave(u_bf16, u_f32, lo, lo + S // 2)
-        for r in range(2):
-            gather(v_f32, 1, list_b, r, 0, S)
+        gather(v_f32, 1, list_b, 1, 0, S)
+        gather(v_f32, 1, list_b, 2, 0, S // 2)
         quantise(0, u_bf16)
-        gather(v_f32, 1, list_b, 2, 0, S)
+        gather(v_f32, 1, list_b, 2, S // 2, S)
         for lo in (0, S // 2):
             gather(v_f32, 1, list_b, 3, lo, lo + S // 2)
         spare = banks[3]

from contextlib import ExitStack

import concourse.mybir as mybir
from concourse.masks import make_identity

F32 = mybir.dt.float32
BF16 = mybir.dt.bfloat16
I32 = mybir.dt.int32
U32 = mybir.dt.uint32
U16 = mybir.dt.uint16
U8 = mybir.dt.uint8
FP4X4 = mybir.dt.float4_e2m1fn_x4
E4M3X4 = mybir.dt.float8_e4m3fn_x4
E5M2X4 = mybir.dt.float8_e5m2_x4
MULT = mybir.AluOpType.mult
ADD = mybir.AluOpType.add
COPY = mybir.ActivationFunctionType.Copy

N, K, T, S = 512, 512, 1024, 512
P = 128
PACK = 4
BANK = 512
LATE = 16
FLOPS = 2 * 2 * N * K * S


def tile_moe_experts_input_gradient_two_kernel(
    tc, g, wa_words, wa_scales, wb_words, wb_scales, ga, gb, run, offs, offs2, out
):
    nc = tc.nc
    with ExitStack() as ctx:
        keep = ctx.enter_context(tc.tile_pool(name="keep", bufs=1))
        psum = ctx.enter_context(tc.psum_pool(name="psum", bufs=1))

        def sb(name, shape, dtype, tag=None):
            return keep.tile(shape, dtype, name=name, tag=tag or name, align_bytes=64)

        list_a = keep.tile([P, S // 16], U16, name="list_a")
        list_b = keep.tile([P, S // 16], U16, name="list_b")
        g_rows = [sb("g_rows%d" % r, [P, T], F32) for r in range(PACK)]
        run_rows = [sb("run_rows%d" % kt, [P, T], F32) for kt in range(K // P)]
        gate_cols = [sb("gate_cols%d" % e, [P, PACK], F32) for e in range(2)]
        gate = [sb("gate%d" % e, [P, S], F32) for e in range(2)]
        wa_sb = sb("wa_sb", [P, 2 * K], U8)
        wb_sb = sb("wb_sb", [P, K], U32)
        w_scales = sb("w_scales", [P, 2 * K], U8)
        identity = sb("identity", [P, P], F32)
        places = {i: sb("places%d" % i, [P, T], F32) for i in (0, 2, 3)}
        v0_plain = sb("v0_plain", [P, S], F32)
        v0_gated = sb("v0_gated", [P, S], F32)
        u_f32 = sb("u_f32", [P, PACK * S], F32)
        v_f32 = sb("v_f32", [P, PACK * S + S // 2], F32)
        u_bf16 = v_f32[:, 2 * S + S // 2 :].bitcast(BF16)
        v_bf16 = sb("v_bf16", [P, PACK * S], BF16)
        codes = [sb("codes%d" % e, [P, S], U32) for e in range(2)]
        scales = [sb("scales%d" % e, [P, S], U8) for e in range(2)]
        shared = sb("shared", [P, 2, S - LATE + BANK], F32)
        late_part = sb("late_part", [P, 2, LATE], F32)
        staged = {}
        for e in range(2):
            for kt in range(K // P):
                if e == 0 and kt in (1, 2):
                    staged[e, kt] = v_f32[:, (kt - 1) * S : kt * S]
                elif kt == 3:
                    staged[e, kt] = shared[:, e, 0:S]
                else:
                    staged[e, kt] = sb("staged%d_%d" % (e, kt), [P, S], F32)[:]
        turned = [[sb("turned%d_%d" % (kt, h), [P, BANK], F32)[:] for h in range(2)] for kt in range(K // P)]
        turned[0][1] = shared[:, 0, S - LATE :]
        result = [[sb("result%d_%d" % (kt, h), [P, BANK], F32) for h in range(2)] for kt in range(K // P)]

        banks = [[psum.tile([P, BANK], F32, name="bank%d_%d" % (kt, h)) for h in range(2)] for kt in range(K // P)]

        nc.vector.memset(w_scales[:].bitcast(U32), 0)
        make_identity(nc, identity[:])
        nc.gpsimd.memset(places[0][:], 0.0)
        for i in (2, 3):
            nc.vector.memset(places[i][:], 0.0)

        g_view = g.rearrange("(p r) t -> r p t", r=PACK)
        nc.scalar.dma_start(gate_cols[0][:], ga.rearrange("o (p c) -> (o p) c", c=PACK))
        nc.scalar.dma_start(gate_cols[1][:], gb.rearrange("o (p c) -> (o p) c", c=PACK))
        nc.sync.dma_start(list_b[:], offs2)
        nc.sync.dma_start(g_rows[0][:], g_view[0])
        nc.sync.dma_start(list_a[:], offs)
        for r in range(1, PACK):
            nc.sync.dma_start(g_rows[r][:], g_view[r])

        def load_scales(e, dram):
            rows = dram[0].bitcast(I32).rearrange("(q r) c -> r q c", r=4)
            plane = w_scales[:, e * K : (e + 1) * K].bitcast(I32)
            for r in range(4):
                nc.sync.dma_start(plane[r:P:32, :], rows[r])

        nc.sync.dma_start(wa_sb[:].bitcast(I32), wa_words[0].bitcast(I32))
        load_scales(0, wa_scales)
        nc.sync.dma_start(wb_sb[:].bitcast(I32), wb_words[0].rearrange("p n r -> p (n r)").bitcast(I32))
        load_scales(1, wb_scales)
        for kt in range(K // P):
            nc.sync.dma_start(run_rows[kt][:], run[kt * P : (kt + 1) * P, :])

        def spread_gate(e):
            bank = banks[0][e]
            for c in range(PACK):
                nc.tensor.transpose(
                    bank[:, c * P : (c + 1) * P], gate_cols[e][:, c : c + 1].to_broadcast([P, P]), identity[:]
                )
            nc.scalar.copy(
                gate[e][:].rearrange("p (n c) -> p n c", c=PACK), bank[:].rearrange("p (c n) -> p n c", c=PACK)
            )

        def gather(dst, e, lst, r, lo, hi):
            nc.vector.tensor_tensor(
                dst[:, r * S + lo : r * S + hi],
                g_rows[r][:].indirect(lst[:, lo // 16 : hi // 16]),
                gate[e][:, lo:hi],
                MULT,
            )

        def weave(dst, src, lo, hi):
            a, b = lo // 4, hi // 4
            nc.scalar.copy(
                dst.rearrange("p (c i r) -> p c r i", i=4, r=PACK)[:, a:b],
                src[:, : PACK * S].rearrange("p (r c i) -> p c r i", i=4, r=PACK)[:, a:b],
            )

        def quantise(e, src):
            nc.vector.quantize_mx(out=codes[e][:].bitcast(E5M2X4), scales=scales[e][:], in_=src)

        def product(e, kt, bank):
            if e == 0:
                w = wa_sb[:, 2 * kt * P : 2 * (kt + 1) * P].bitcast(FP4X4)
            else:
                w = wb_sb[:, kt * P : (kt + 1) * P].bitcast(E4M3X4)
            nc.tensor.matmul_mx(
                out=bank[:],
                lhsT=w,
                lhsT_scale=w_scales[:, e * K + kt * P : e * K + (kt + 1) * P],
                rhs=codes[e][:].bitcast(E5M2X4),
                rhs_scale=scales[e][:],
                start=True,
                stop=True,
            )

        def stage(e, kt, bank):
            product(e, kt, bank)
            nc.scalar.copy(staged[e, kt], bank[:])

        def stage_but_last(e, bank):
            nc.scalar.copy(staged[e, 3][:, : S - LATE], bank[:, : S - LATE])
            nc.scalar.copy(late_part[:, e, :], bank[:, S - LATE :])

        def scatter(e, kt):
            lst = list_a if e == 0 else list_b
            nc.vector.tensor_copy(places[4 if (e, kt) == (0, 2) else 2 * e + kt % 2][:].indirect(lst[:]), staged[e, kt])

        def add_turned(kt, src, ident, first, last):
            for h in range(2):
                for b in range(4):
                    col = h * BANK + b * P
                    nc.tensor.matmul(
                        banks[kt][h][:, b * P : (b + 1) * P],
                        src[:, col : col + P],
                        ident[:],
                        is_transpose=True,
                        start=(first and b == 0),
                        stop=(last and b == 3),
                    )

        def identity_over(tag):
            copy = sb("identity_" + tag, [P, P], F32, tag=tag)
            nc.scalar.copy(copy[:], identity[:])
            return copy

        def turn_back(kt):
            for h in range(2):
                nc.scalar.copy(turned[kt][h], banks[kt][h][:])
                for b in range(4):
                    nc.tensor.transpose(
                        banks[kt][h][:, b * P : (b + 1) * P], turned[kt][h][:, b * P : (b + 1) * P], identity[:]
                    )

        def store(kt):
            for h in range(2):
                nc.scalar.copy(result[kt][h][:], banks[kt][h][:])
                nc.sync.dma_start(out[kt * P : (kt + 1) * P, h * BANK : (h + 1) * BANK], result[kt][h][:])

        spread_gate(0)
        spread_gate(1)
        nc.vector.tensor_copy(v0_plain[:], g_rows[0][:].indirect(list_b[:]))
        there, back = banks[1]
        for c in range(PACK):
            nc.tensor.transpose(there[:, c * P : (c + 1) * P], v0_plain[:, c:S:PACK], identity[:])
        for c in range(PACK):
            nc.scalar.activation(
                v0_gated[:, c * P : (c + 1) * P], there[:, c * P : (c + 1) * P], COPY, scale=gate_cols[1][:, c : c + 1]
            )
        for c in range(PACK):
            nc.tensor.transpose(back[:, c * P : (c + 1) * P], v0_gated[:, c * P : (c + 1) * P], identity[:])
        nc.scalar.copy(
            v_f32[:, 0:S].rearrange("p (n c) -> p n c", c=PACK), back[:].rearrange("p (c n) -> p n c", c=PACK)
        )
        places[1] = sb("places1", [P, T], F32, tag="v0_plain")
        places[4] = sb("places4", [P, T], F32, tag="v0_gated")
        for i in (1, 4):
            nc.gpsimd.memset(places[i][:], 0.0)
        for r in range(2):
            gather(u_f32, 0, list_a, r, 0, S)
        for lo in (0, S // 2):
            for r in (2, 3):
                gather(u_f32, 0, list_a, r, lo, lo + S // 2)
            weave(u_bf16, u_f32, lo, lo + S // 2)
        gather(v_f32, 1, list_b, 1, 0, S)
        gather(v_f32, 1, list_b, 2, 0, S // 2)
        quantise(0, u_bf16)
        gather(v_f32, 1, list_b, 2, S // 2, S)
        for lo in (0, S // 2):
            gather(v_f32, 1, list_b, 3, lo, lo + S // 2)
        spare = banks[3]
        stage(0, 0, spare[0])
        product(0, 1, spare[1])
        product(0, 2, spare[0])
        for lo in (0, S // 2):
            weave(v_bf16[:], v_f32, lo, lo + S // 2)
        scatter(0, 0)
        quantise(1, v_bf16[:])
        nc.scalar.copy(staged[0, 1], spare[1][:])
        scatter(0, 1)
        nc.scalar.copy(staged[0, 2], spare[0][:])
        product(0, 3, spare[1])
        stage_but_last(0, spare[1])
        for kt in range(3):
            add_turned(kt, run_rows[kt], identity, True, False)
        add_turned(0, places[0], identity, False, False)
        for kt in range(3):
            stage(1, kt, spare[kt % 2])
        product(1, 3, spare[1])
        stage_but_last(1, spare[1])
        ident = identity_over("wb_sb")
        scatter(0, 2)
        add_turned(1, places[1], ident, False, False)
        add_turned(2, places[4], ident, False, False)
        scatter(1, 0)
        add_turned(3, run_rows[3], identity, True, False)
        ident = identity_over("run_rows3")
        scatter(1, 1)
        add_turned(0, places[2], ident, False, True)
        scatter(1, 2)
        turn_back(0)
        ident = identity_over("turned0_0")
        nc.scalar.copy(shared[:, :, S - LATE : S], late_part[:])
        store(0)
        add_turned(1, places[3], ident, False, True)
        scatter(0, 3)
        scatter(1, 3)
        turn_back(1)
        ident = identity_over("turned1_0")
        store(1)
        add_turned(2, places[2], ident, False, True)
        turn_back(2)
        ident = identity_over("turned2_0")
        store(2)
        add_turned(3, places[1], ident, False, True)
        turn_back(3)
        for h, lo, hi, queue in ((0, 0, BANK, nc.sync), (1, 0, BANK // 2, nc.scalar), (1, BANK // 2, BANK, nc.sync)):
            cols = slice(h * BANK + lo, h * BANK + hi)
            nc.vector.tensor_tensor(result[3][h][:, lo:hi], banks[3][h][:, lo:hi], places[3][:, cols], ADD)
            queue.dma_start(out[3 * P : 4 * P, cols], result[3][h][:, lo:hi])
